import numpy as np
import ml_dtypes


def mxq(x, axis, fmt="e4m3"):
    dtype, down = {"e4m3": (ml_dtypes.float8_e4m3fn, 7), "e5m2": (ml_dtypes.float8_e5m2, 14)}[fmt]
    v = np.moveaxis(np.asarray(x, np.float32).astype(ml_dtypes.bfloat16).astype(np.float64), axis, -1)
    blocks = v.reshape(v.shape[:-1] + (-1, 32))
    amax = np.abs(blocks).max(-1, keepdims=True)
    byte = np.maximum(np.where(amax > 0, np.frexp(amax)[1] - 1 + 127, 0) - down, 1)
    scale = np.exp2(byte - 127.0)
    codes = (blocks / scale).astype(np.float32).astype(dtype).astype(np.float64)
    return np.moveaxis((codes * scale).reshape(v.shape), -1, axis)


WIDE = False


def mx_kscale(k):
    if not WIDE:
        return np.ones(k)
    levels = np.array([10, -10, 5, -5, 0])
    if k % 512:
        return np.exp2(np.random.permutation(np.resize(levels, k // 32))).repeat(32)
    a = np.empty((k // 512, 16))
    for p in range(k // 512):
        a[p, :8] = np.random.permutation(np.resize(levels, 8))
        for g in range(8):
            far = levels[np.abs(levels - a[p, g]) >= 10]
            a[p, g + 8] = far[np.random.randint(len(far))]
    return np.exp2(a.ravel()).repeat(32)


def f64(x):
    return np.asarray(x).astype(np.float64)


def striped(idx):
    return np.tile(idx.reshape(-1, 16).T, (8, 1)).astype(np.uint16)


def unstriped(offs):
    return offs[:16].T.reshape(-1).astype(np.int64)


def pack_weight(w):
    k, n = w.shape
    w = f64(np.asarray(w, np.float32).astype(ml_dtypes.bfloat16)).reshape(k // 32, 32, n)
    amax = np.abs(w).max(1)
    byte = np.clip(np.where(amax > 0, np.frexp(amax)[1] - 1 + 127 - 7, 1), 1, 254)
    scaled = (w * np.exp2(127.0 - byte)[:, None, :]).reshape(k, n).astype(np.float32)
    words = np.ascontiguousarray(scaled.reshape(k // 512, 128, 4, n).transpose(0, 1, 3, 2)).astype(ml_dtypes.float8_e4m3fn).view(np.uint8)
    return words, np.ascontiguousarray(byte.astype(np.uint8).reshape(k // 512, 16, n))


def unpack_weight(words, scales):
    g, p, n, _ = words.shape
    vals = np.ascontiguousarray(words).view(ml_dtypes.float8_e4m3fn).astype(np.float64) * np.repeat(np.exp2(scales.astype(np.float64) - 127.0), 8, axis=1)[..., None]
    return vals.transpose(0, 1, 3, 2).reshape(g * 512, n)


def sigmoid(v):
    return 1.0 / (1.0 + np.exp(-np.maximum(v, -700.0)))


K, T, S, N, H = 512, 1024, 512, 256, 512


def setup_inputs():
    n = np.random.standard_normal
    s = mx_kscale(K)[:, None]
    u = mx_kscale(H)
    packed_xT = pack_weight(n((K, T)) * s)
    return {
        "x_words": packed_xT[0],
        "x_scales": packed_xT[1],
        "w1": (n((K, H)) / np.sqrt(K) / s).astype(np.float32),
        "w2": (n((K, H)) / np.sqrt(K) / s).astype(np.float32),
        "unit": (np.random.uniform(0.6, 1.4, (H, 1)) * u[:, None]).astype(np.float32),
        "w3": (n((H, N)) / np.sqrt(H) / u[:, None]).astype(np.float32),
        "offs": striped(np.random.permutation(T)[:S]),
        "p1": striped(np.random.permutation(S)),
        "p2": striped(np.random.permutation(S)),
        "p3": striped(np.random.permutation(S)),
    }


def reference(x_words, x_scales, w1, w2, unit, w3, offs, p1, p2, p3):
    xq = unpack_weight(x_words, x_scales)[:, unstriped(offs)]
    y = mxq(f64(w1), 0, "e4m3").T @ xq
    yw = mxq(f64(w2), 0, "e4m3").T @ xq
    dec = sigmoid(yw)
    y1 = y[:, unstriped(p1)]
    up1 = y + dec * y1
    ap = dec[:, unstriped(p1)]
    dec2 = dec * ap
    x12 = up1[:, unstriped(p2)]
    up2_ = up1 + dec2 * x12
    a3 = dec2[:, unstriped(p3)]
    hid = f64(unit) * (up2_ - (1.5 * a3))
    return mxq(f64(w3), 0, "e4m3").T @ mxq(hid, 0, "e4m3")

from contextlib import ExitStack

import concourse.mybir as mybir
from concourse.masks import make_identity

K, T, S, N, H = 512, 1024, 512, 256, 512
FLOPS = 2 * K * H * S * 2 + 2 * H * N * S

F32 = mybir.dt.float32
BF16 = mybir.dt.bfloat16
I32 = mybir.dt.int32
U32 = mybir.dt.uint32
U16 = mybir.dt.uint16
U8 = mybir.dt.uint8
FP8X4 = mybir.dt.float8_e4m3fn_x4
MULT = mybir.AluOpType.mult
ADD = mybir.AluOpType.add
COPY = mybir.ActivationFunctionType.Copy
SIGMOID = mybir.ActivationFunctionType.Sigmoid

P = 128
PACK = 4
TILES = H // P
BLOCKS = S // P
SPARE = 16
HALF = S // 2
SCALAR_FETCH = (0, 3)


def tile_picked_yptrjmp_sum_p_kernel(
    tc, x_words, x_scales, w1, w2, unit, w3, offs, p1, p2, p3, out
):
    nc = tc.nc
    with ExitStack() as ctx:
        keep = ctx.enter_context(tc.tile_pool(name="keep", bufs=1))
        psum = ctx.enter_context(tc.psum_pool(name="psum", bufs=1))

        def load_list(name, src):
            tile = keep.tile([P, S // 16], U16, name=name)
            nc.sync.dma_start(tile[:], src)
            return tile

        def load_columns(name, w, c0, c1):
            raw = keep.tile([P, PACK, c1 - c0], F32, name=name)
            nc.sync.dma_start(out=raw[:], in_=w[:, c0:c1].rearrange("(p k) c -> p k c", k=PACK))
            return raw

        scale_table = keep.tile([P, T], U8, name="scale_table", align_bytes=64)
        nc.vector.memset(scale_table[:].bitcast(I32), 0)
        for q in range(4):
            nc.scalar.dma_start(
                out=scale_table[32 * q : 32 * q + 4, :].bitcast(I32),
                in_=x_scales[0, 4 * q : 4 * q + 4, :].bitcast(I32),
            )
        offs_t = load_list("offs_t", offs)
        word_table = keep.tile([P, T], I32, name="word_table", align_bytes=64)
        nc.sync.dma_start(out=word_table[:], in_=x_words[0].rearrange("p n t -> p (n t)").bitcast(I32))

        raw2, raw1 = {}, {}
        raw2[0] = load_columns("raw2_0", w2, 0, P)[:]
        raw1[0] = load_columns("raw1_0", w1, 0, P)[:]
        p1_t = load_list("p1_t", p1)
        raw2[1] = load_columns("raw2_1", w2, P, 2 * P)[:]
        raw1[1] = load_columns("raw1_1", w1, P, 2 * P)[:]
        p2_t = load_list("p2_t", p2)
        p3_t = load_list("p3_t", p3)
        rest2 = load_columns("raw2_rest", w2, 2 * P, H)
        rest1 = load_columns("raw1_rest", w1, 2 * P, H)
        for t in (2, 3):
            raw2[t] = rest2[:, :, (t - 2) * P : (t - 1) * P]
            raw1[t] = rest1[:, :, (t - 2) * P : (t - 1) * P]
        raw3 = load_columns("raw3", w3, 0, N)

        unit_t = keep.tile([P, TILES], F32, name="unit_t")
        with nc.allow_non_contiguous_dma(reason="one value a partition and tile"):
            nc.gpsimd.dma_start(out=unit_t[:], in_=unit.rearrange("(t p) o -> p (t o)", p=P))
        ident = keep.tile([P, P], F32, name="ident")
        make_identity(nc, ident[:])

        def window(name):
            tile = keep.tile([P, S + SPARE], F32, name=name)
            nc.gpsimd.memset(tile[:, S:], 0.0)
            return tile

        y = [window("y%d" % t) for t in range(TILES)]
        dec = [window("dec%d" % t) for t in range(TILES)]
        up1 = [window("up1_%d" % t) for t in range(TILES)]
        pull = [window("pull%d" % t) for t in range(TILES)]
        dec2 = [keep.tile([P, S], F32, name="dec2_%d" % t) for t in range(TILES)]

        x_bytes = keep.tile([P, S], U8, name="x_bytes", align_bytes=64)
        x_codes = keep.tile([P, S], U32, name="x_codes", align_bytes=64)

        def gather_nodes(h):
            cols = slice(h * HALF, (h + 1) * HALF)
            entries = offs_t[:, h * HALF // 16 : (h + 1) * HALF // 16]
            nc.vector.tensor_copy(x_codes[:, cols], word_table[:].bitcast(U32).indirect(entries))
            nc.vector.tensor_copy(x_bytes[:, cols], scale_table[:].indirect(entries))

        def round_weights(name, tag, raw, copy):
            width = raw.shape[2]
            grouped = keep.tile([P, width, PACK], BF16, name=name, tag=tag, align_bytes=64)
            copy(
                out=grouped[:].rearrange("p (c i) k -> p c k i", i=4),
                in_=raw.rearrange("p k (c i) -> p c k i", i=4),
            )
            return grouped

        def quantize(name, grouped):
            width = grouped.shape[1]
            codes = keep.tile([P, width], U32, name=name + "_codes", align_bytes=64)
            scales = keep.tile([P, width], U8, name=name + "_scales", align_bytes=64)
            nc.vector.quantize_mx(
                out=codes[:].bitcast(FP8X4), scales=scales[:], in_=grouped[:].rearrange("p c k -> p (c k)")
            )
            return codes, scales

        w1q, w2q = {}, {}

        def prepare(t, copy):
            w2q[t] = quantize("w2q%d" % t, round_weights("w2_bf16_%d" % t, "w2_bf16", raw2[t], copy))
            w1q[t] = quantize("w1q%d" % t, round_weights("w1_bf16_%d" % t, "w1_bf16", raw1[t], copy))

        def first_product(name, weights, cols):
            codes, scales = weights
            bank = psum.tile([P, cols.stop - cols.start], F32, name=name, tag="product", bufs=4)
            nc.tensor.matmul_mx(
                out=bank[:],
                lhsT=codes[:].bitcast(FP8X4),
                lhsT_scale=scales[:],
                rhs=x_codes[:, cols].bitcast(FP8X4),
                rhs_scale=x_bytes[:, cols],
                start=True,
                stop=True,
            )
            return bank

        def products(t, cols):
            name = "%d_%d" % (t, cols.start)
            nc.scalar.activation(dec[t][:, cols], first_product("yw" + name, w2q[t], cols)[:], SIGMOID)
            nc.scalar.activation(
                y[t][:, cols], first_product("y" + name, w1q[t], cols)[:], COPY, scale=unit_t[:, t : t + 1]
            )

        partner = [keep.tile([P, S], F32, name="partner%d" % t) for t in range(TILES)]
        carried = [keep.tile([P, S], F32, name="carried%d" % t) for t in range(TILES)]
        second = [keep.tile([P, S], F32, name="second%d" % t) for t in range(TILES)]
        pulled = [keep.tile([P, S], F32, name="pulled%d" % t) for t in range(TILES)]
        hid_rows = [keep.tile([P, 2, P, 2], BF16, name="hid_rows%d" % b, align_bytes=64) for b in range(BLOCKS)]

        def fetch_partner(t):
            if t in SCALAR_FETCH:
                nc.scalar.activation(partner[t][:], dec[t][:].indirect(p1_t[:]), COPY)
            else:
                nc.sync.dma_start(out=partner[t][:], in_=dec[t][:, :S])

        def carry(t):
            nc.vector.tensor_tensor(carried[t][:], y[t][:].indirect(p1_t[:]), dec[t][:, :S], MULT)

        def decay(t):
            if t in SCALAR_FETCH:
                nc.vector.tensor_tensor(dec2[t][:], dec[t][:, :S], partner[t][:], MULT)
            else:
                nc.vector.tensor_tensor(dec2[t][:], dec[t][:].indirect(p1_t[:]), partner[t][:], MULT)

        def first_jump(t):
            nc.vector.tensor_tensor(up1[t][:, :S], y[t][:, :S], carried[t][:], ADD)

        def scale_pull(t):
            nc.vector.tensor_scalar(pull[t][:, :S], dec2[t][:], unit_t[:, t : t + 1], -1.5, MULT, MULT)

        def compare(t):
            nc.scalar.activation(pulled[t][:], pull[t][:].indirect(p3_t[:]), COPY)

        def second_jump(t, cols):
            entries = p2_t[:, cols.start // 16 : cols.stop // 16]
            nc.vector.tensor_tensor(second[t][:, cols], up1[t][:].indirect(entries), dec2[t][:, cols], MULT)

        def hidden(t, b0, b1, tag, bufs):
            bank = psum.tile([P, b1 - b0, P], F32, name="hid_bank%d_%d" % (t, b0), tag=tag, bufs=bufs)
            terms = (up1[t], pulled[t], second[t])
            for a, term in enumerate(terms):
                for b in range(b0, b1):
                    nc.tensor.matmul(
                        bank[:, b - b0, :],
                        lhsT=term[:, b * P : (b + 1) * P],
                        rhs=ident[:],
                        is_transpose=True,
                        start=(a == 0 and b == b0),
                        stop=(a == len(terms) - 1 and b == b1 - 1),
                    )
            for b in range(b0, b1):
                nc.scalar.copy(
                    out=hid_rows[b][:, :, 32 * t : 32 * (t + 1), :],
                    in_=bank[:, b - b0, :].rearrange("j (p u e) -> j u p e", u=2, e=2),
                )

        def last_product(b):
            hid_words = hid_rows[b][:].rearrange("j u p e -> j u (p e)").bitcast(F32)
            back = psum.tile([P, 2, P], F32, name="back%d" % b, tag="back", bufs=2)
            for u in range(2):
                nc.tensor.transpose(back[:, u, :], hid_words[:, u, :], ident[:])
            hid_bf16 = keep.tile([P, P, PACK], BF16, name="hid_bf16_%d" % b, align_bytes=64)
            nc.scalar.copy(out=hid_bf16[:].bitcast(F32), in_=back[:].rearrange("p u j -> p j u"))
            hid_codes, hid_scales = quantize("hidq%d" % b, hid_bf16)
            bank = psum.tile([P, 2, P], F32, name="out_bank%d" % b, tag="hidden", bufs=2)
            for m in range(2):
                nc.tensor.matmul_mx(
                    out=bank[:, m, :],
                    lhsT=w3_codes[:, m * P : (m + 1) * P].bitcast(FP8X4),
                    lhsT_scale=w3_scales[:, m * P : (m + 1) * P],
                    rhs=hid_codes[:].bitcast(FP8X4),
                    rhs_scale=hid_scales[:],
                    start=True,
                    stop=True,
                )
            result = keep.tile([P, 2, P], F32, name="result%d" % b)
            nc.vector.tensor_copy(out=result[:], in_=bank[:])
            nc.sync.dma_start(
                out=out[:, b * P : (b + 1) * P].rearrange("(m p) j -> p m j", p=P), in_=result[:]
            )

        whole = slice(0, S)
        last = TILES - 1
        gather_nodes(0)
        prepare(0, nc.scalar.copy)
        gather_nodes(1)
        products(0, slice(0, HALF))
        products(0, slice(HALF, S))
        prepare(1, nc.vector.tensor_copy)
        fetch_partner(0)
        carry(0)
        products(1, whole)
        fetch_partner(1)
        decay(0)
        prepare(2, nc.scalar.copy)
        for t in range(TILES):
            if t > 0:
                carry(t)
            if t == 1:
                prepare(3, nc.scalar.copy)
            if t == 2:
                w3_codes, w3_scales = quantize(
                    "w3q", round_weights("w3_bf16", "w3_bf16", raw3[:], nc.scalar.copy)
                )
            if t == 0:
                scale_pull(t)
                compare(t)
            first_jump(t)
            if t + 2 < TILES:
                products(t + 2, whole)
                fetch_partner(t + 2)
            if t > 0:
                hidden(t - 1, 0, BLOCKS, "hidden", 2)
            if t < last:
                decay(t + 1)
                second_jump(t, whole)
                scale_pull(t + 1)
                compare(t + 1)
        for b in range(BLOCKS):
            second_jump(last, slice(b * P, (b + 1) * P))
            hidden(last, b, b + 1, "product", 4)
        for b in range(BLOCKS):
            last_product(b)
